import numpy as np
import ml_dtypes

BF16 = ml_dtypes.bfloat16


def bf(x):
    return np.asarray(x, np.float32).astype(BF16)


def f32(x):
    return np.asarray(x, np.float32)


def f64(x):
    return np.asarray(x).astype(np.float64)


def striped(idx):
    return np.tile(idx.reshape(-1, 16).T, (8, 1))


def rows(idx, k):
    return np.tile(idx, (k, 1))


def look(tab, idx):
    return np.take_along_axis(f64(tab), rows(idx, len(tab)), axis=1)


K, S, V, N = 512, 2048, 1024, 1024


def setup_inputs():
    return {"tab": f32(np.random.standard_normal((2, K, S))), "offs": striped(np.random.permutation(S)[:N])}


def reference(tab, offs):
    idx = offs[:16].T.reshape(-1)
    x = ((look(tab[0], idx) - 0.125) * 1.5) * (np.maximum(look(tab[1], idx), 0.0))
    return x

@@ -1,0 +1,45 @@
+import concourse.mybir as mybir
+
+F32, U16 = mybir.dt.float32, mybir.dt.uint16
+RELU = mybir.ActivationFunctionType.Relu
+SUBTRACT, MULT = mybir.AluOpType.subtract, mybir.AluOpType.mult
+SHIFT, SCALE = 0.125, 1.5
+P = 128
+LAST_PIECES = 4
+
+
+def tile_lookup_vg_nrmrelu_out_kernel(tc, tab, offs, out):
+    nc = tc.nc
+    rows, places = tab.shape[1], tab.shape[2]
+    entries = out.shape[1]
+    with (
+        tc.tile_pool(name="lists", bufs=1) as lists,
+        tc.tile_pool(name="windows", bufs=rows // P) as windows,
+        tc.tile_pool(name="picked", bufs=rows // P) as picked,
+    ):
+        offsets = lists.tile([P, entries // 16], U16, name="offsets")
+        values, gates = [], []
+        for block in range(rows // P):
+            block_rows = slice(block * P, (block + 1) * P)
+            values.append(windows.tile([P, places], F32, name="values"))
+            gates.append(windows.tile([P, places], F32, name="gates"))
+            nc.sync.dma_start(values[block][:], tab[0, block_rows, :])
+            if block == 0:
+                nc.sync.dma_start(offsets[:], offs)
+            nc.sync.dma_start(gates[block][:], tab[1, block_rows, :])
+
+        for block in range(rows // P):
+            scaled = picked.tile([P, entries], F32, name="scaled")
+            opened = picked.tile([P, entries], F32, name="opened")
+            product = picked.tile([P, entries], F32, name="product")
+            nc.vector.tensor_scalar(
+                scaled[:], values[block][:].indirect(offsets[:]), SHIFT, SCALE, op0=SUBTRACT, op1=MULT
+            )
+            pieces = LAST_PIECES if block == rows // P - 1 else 1
+            piece = entries // pieces
+            for start in range(0, entries, piece):
+                columns = slice(start, start + piece)
+                piece_offsets = offsets[:, start // 16 : (start + piece) // 16]
+                nc.scalar.activation(opened[:, columns], gates[block][:].indirect(piece_offsets), RELU)
+                nc.vector.tensor_tensor(product[:, columns], scaled[:, columns], opened[:, columns], MULT)
+                nc.sync.dma_start(out[block * P : (block + 1) * P, columns], product[:, columns])

@@ -5,41 +5,67 @@ RELU = mybir.ActivationFunctionType.Relu
 SUBTRACT, MULT = mybir.AluOpType.subtract, mybir.AluOpType.mult
 SHIFT, SCALE = 0.125, 1.5
 P = 128
-LAST_PIECES = 4
+SECOND_LAST_PIECES = (512, 512)
+LAST_PIECES = (448, 256, 192, 128)
 
 
 def tile_lookup_vg_nrmrelu_out_kernel(tc, tab, offs, out):
     nc = tc.nc
     rows, places = tab.shape[1], tab.shape[2]
     entries = out.shape[1]
+    blocks = rows // P
+    table = tab.rearrange("h (p b) s -> h b p s", b=blocks)
+    result = out.rearrange("(p b) n -> p (b n)", b=blocks)
     with (
-        tc.tile_pool(name="lists", bufs=1) as lists,
-        tc.tile_pool(name="windows", bufs=rows // P) as windows,
-        tc.tile_pool(name="picked", bufs=rows // P) as picked,
+        tc.tile_pool(name="held", bufs=1) as held,
+        tc.tile_pool(name="windows", bufs=blocks) as windows,
+        tc.tile_pool(name="picked", bufs=blocks) as picked,
     ):
-        offsets = lists.tile([P, entries // 16], U16, name="offsets")
-        values, gates = [], []
-        for block in range(rows // P):
-            block_rows = slice(block * P, (block + 1) * P)
-            values.append(windows.tile([P, places], F32, name="values"))
-            gates.append(windows.tile([P, places], F32, name="gates"))
-            nc.sync.dma_start(values[block][:], tab[0, block_rows, :])
+        offsets = held.tile([P, entries // 16], U16, name="offsets")
+        product = held.tile([P, blocks * entries], F32, name="product")
+        values = [windows.tile([P, places], F32, name="values") for block in range(blocks)]
+        gates = [windows.tile([P, places], F32, name="gates") for block in range(blocks)]
+        scaled = [picked.tile([P, entries], F32, name="scaled") for block in range(blocks)]
+
+        early = blocks - 2
+        for block in range(early):
+            nc.sync.dma_start(values[block][:], table[0, block])
             if block == 0:
                 nc.sync.dma_start(offsets[:], offs)
-            nc.sync.dma_start(gates[block][:], tab[1, block_rows, :])
+            nc.sync.dma_start(gates[block][:], table[1, block])
+        for block in range(early, blocks):
+            nc.sync.dma_start(values[block][:], table[0, block])
+        for block in range(early, blocks):
+            nc.sync.dma_start(gates[block][:], table[1, block])
 
-        for block in range(rows // P):
-            scaled = picked.tile([P, entries], F32, name="scaled")
-            opened = picked.tile([P, entries], F32, name="opened")
-            product = picked.tile([P, entries], F32, name="product")
+        def look_up_values(block):
             nc.vector.tensor_scalar(
-                scaled[:], values[block][:].indirect(offsets[:]), SHIFT, SCALE, op0=SUBTRACT, op1=MULT
+                scaled[block][:], values[block][:].indirect(offsets[:]), SHIFT, SCALE, op0=SUBTRACT, op1=MULT
             )
-            pieces = LAST_PIECES if block == rows // P - 1 else 1
-            piece = entries // pieces
-            for start in range(0, entries, piece):
+
+        def store(first, end):
+            nc.sync.dma_start(result[:, first:end], product[:, first:end])
+
+        def gate(block, pieces, store_each_piece):
+            opened = picked.tile([P, entries], F32, name="opened")
+            start = 0
+            for piece in pieces:
                 columns = slice(start, start + piece)
+                first = block * entries + start
                 piece_offsets = offsets[:, start // 16 : (start + piece) // 16]
                 nc.scalar.activation(opened[:, columns], gates[block][:].indirect(piece_offsets), RELU)
-                nc.vector.tensor_tensor(product[:, columns], scaled[:, columns], opened[:, columns], MULT)
-                nc.sync.dma_start(out[block * P : (block + 1) * P, columns], product[:, columns])
+                nc.vector.tensor_tensor(
+                    product[:, first : first + piece], scaled[block][:, columns], opened[:, columns], MULT
+                )
+                if store_each_piece:
+                    store(first, first + piece)
+                start += piece
+
+        look_up_values(0)
+        for block in range(early):
+            look_up_values(block + 1)
+            gate(block, (entries,), False)
+        look_up_values(blocks - 1)
+        store(0, early * entries)
+        gate(blocks - 2, SECOND_LAST_PIECES, True)
+        gate(blocks - 1, LAST_PIECES, True)

@@ -5,7 +5,7 @@ RELU = mybir.ActivationFunctionType.Relu
 SUBTRACT, MULT = mybir.AluOpType.subtract, mybir.AluOpType.mult
 SHIFT, SCALE = 0.125, 1.5
 P = 128
-SECOND_LAST_PIECES = (512, 512)
+EARLY_PIECES, LATE_PIECE = (512, 256), 256
 LAST_PIECES = (448, 256, 192, 128)
 
 
@@ -14,6 +14,7 @@ def tile_lookup_vg_nrmrelu_out_kernel(tc, tab, offs, out):
     rows, places = tab.shape[1], tab.shape[2]
     entries = out.shape[1]
     blocks = rows // P
+    last = blocks - 1
     table = tab.rearrange("h (p b) s -> h b p s", b=blocks)
     result = out.rearrange("(p b) n -> p (b n)", b=blocks)
     with (
@@ -25,47 +26,52 @@ def tile_lookup_vg_nrmrelu_out_kernel(tc, tab, offs, out):
         product = held.tile([P, blocks * entries], F32, name="product")
         values = [windows.tile([P, places], F32, name="values") for block in range(blocks)]
         gates = [windows.tile([P, places], F32, name="gates") for block in range(blocks)]
-        scaled = [picked.tile([P, entries], F32, name="scaled") for block in range(blocks)]
+        opened = [picked.tile([P, entries], F32, name="opened") for block in range(blocks)]
+        scaled = [picked.tile([P, entries], F32, name="scaled") for block in range(last)]
+        scaled.append(scaled[-1])
 
-        early = blocks - 2
-        for block in range(early):
+        for block in range(blocks):
             nc.sync.dma_start(values[block][:], table[0, block])
             if block == 0:
                 nc.sync.dma_start(offsets[:], offs)
             nc.sync.dma_start(gates[block][:], table[1, block])
-        for block in range(early, blocks):
-            nc.sync.dma_start(values[block][:], table[0, block])
-        for block in range(early, blocks):
-            nc.sync.dma_start(gates[block][:], table[1, block])
 
-        def look_up_values(block):
-            nc.vector.tensor_scalar(
-                scaled[block][:], values[block][:].indirect(offsets[:]), SHIFT, SCALE, op0=SUBTRACT, op1=MULT
+        def look_up_values(block, start, end):
+            window = values[block][:].indirect(offsets[:, start // 16 : end // 16])
+            nc.vector.tensor_scalar(scaled[block][:, start:end], window, SHIFT, SCALE, op0=SUBTRACT, op1=MULT)
+
+        def gate(block, start, end):
+            window = gates[block][:].indirect(offsets[:, start // 16 : end // 16])
+            nc.scalar.activation(opened[block][:, start:end], window, RELU)
+            nc.vector.tensor_tensor(
+                product[:, block * entries + start : block * entries + end],
+                scaled[block][:, start:end],
+                opened[block][:, start:end],
+                MULT,
             )
 
-        def store(first, end):
-            nc.sync.dma_start(result[:, first:end], product[:, first:end])
+        def store(block, start, end):
+            columns = slice(block * entries + start, block * entries + end)
+            nc.sync.dma_start(result[:, columns], product[:, columns])
 
-        def gate(block, pieces, store_each_piece):
-            opened = picked.tile([P, entries], F32, name="opened")
-            start = 0
-            for piece in pieces:
-                columns = slice(start, start + piece)
-                first = block * entries + start
-                piece_offsets = offsets[:, start // 16 : (start + piece) // 16]
-                nc.scalar.activation(opened[:, columns], gates[block][:].indirect(piece_offsets), RELU)
-                nc.vector.tensor_tensor(
-                    product[:, first : first + piece], scaled[block][:, columns], opened[:, columns], MULT
-                )
-                if store_each_piece:
-                    store(first, first + piece)
-                start += piece
+        look_up_values(0, 0, entries)
+        for block in range(last - 1):
+            look_up_values(block + 1, 0, entries)
+            gate(block, 0, entries)
+        store(0, 0, (last - 1) * entries)
 
-        look_up_values(0)
-        for block in range(early):
-            look_up_values(block + 1)
-            gate(block, (entries,), False)
-        look_up_values(blocks - 1)
-        store(0, early * entries)
-        gate(blocks - 2, SECOND_LAST_PIECES, True)
-        gate(blocks - 1, LAST_PIECES, True)
+        start = 0
+        for piece in EARLY_PIECES:
+            gate(last - 1, start, start + piece)
+            start += piece
+        store(last - 1, 0, start)
+        look_up_values(last, 0, start)
+        gate(last - 1, start, start + LATE_PIECE)
+        store(last - 1, start, start + LATE_PIECE)
+        look_up_values(last, start, start + LATE_PIECE)
+
+        start = 0
+        for piece in LAST_PIECES:
+            gate(last, start, start + piece)
+            store(last, start, start + piece)
+            start += piece

@@ -5,8 +5,8 @@ RELU = mybir.ActivationFunctionType.Relu
 SUBTRACT, MULT = mybir.AluOpType.subtract, mybir.AluOpType.mult
 SHIFT, SCALE = 0.125, 1.5
 P = 128
-EARLY_PIECES, LATE_PIECE = (512, 256), 256
-LAST_PIECES = (448, 256, 192, 128)
+EARLY_PIECES, LATE_PIECE = (512,), 512
+LAST_PIECES = (256, 256, 256, 128, 128)
 
 
 def tile_lookup_vg_nrmrelu_out_kernel(tc, tab, offs, out):
@@ -64,10 +64,9 @@ def tile_lookup_vg_nrmrelu_out_kernel(tc, tab, offs, out):
         for piece in EARLY_PIECES:
             gate(last - 1, start, start + piece)
             start += piece
-        store(last - 1, 0, start)
         look_up_values(last, 0, start)
         gate(last - 1, start, start + LATE_PIECE)
-        store(last - 1, start, start + LATE_PIECE)
+        store(last - 1, 0, entries)
         look_up_values(last, start, start + LATE_PIECE)
 
         start = 0

@@ -6,7 +6,7 @@ SUBTRACT, MULT = mybir.AluOpType.subtract, mybir.AluOpType.mult
 SHIFT, SCALE = 0.125, 1.5
 P = 128
 EARLY_PIECES, LATE_PIECE = (512,), 512
-LAST_PIECES = (256, 256, 256, 128, 128)
+LAST_PIECES = (320, 256, 192, 128, 128)
 
 
 def tile_lookup_vg_nrmrelu_out_kernel(tc, tab, offs, out):

@@ -1,11 +1,11 @@
 import concourse.mybir as mybir
 
 F32, U16 = mybir.dt.float32, mybir.dt.uint16
-RELU = mybir.ActivationFunctionType.Relu
+COPY, RELU = mybir.ActivationFunctionType.Copy, mybir.ActivationFunctionType.Relu
 SUBTRACT, MULT = mybir.AluOpType.subtract, mybir.AluOpType.mult
 SHIFT, SCALE = 0.125, 1.5
 P = 128
-EARLY_PIECES, LATE_PIECE = (512,), 512
+PAIR = 2
 LAST_PIECES = (320, 256, 192, 128, 128)
 
 
@@ -13,9 +13,10 @@ def tile_lookup_vg_nrmrelu_out_kernel(tc, tab, offs, out):
     nc = tc.nc
     rows, places = tab.shape[1], tab.shape[2]
     entries = out.shape[1]
+    half = entries // 2
     blocks = rows // P
     last = blocks - 1
-    table = tab.rearrange("h (p b) s -> h b p s", b=blocks)
+    table = tab.rearrange("h (p b) s -> h p (b s)", b=blocks)
     result = out.rearrange("(p b) n -> p (b n)", b=blocks)
     with (
         tc.tile_pool(name="held", bufs=1) as held,
@@ -23,18 +24,27 @@ def tile_lookup_vg_nrmrelu_out_kernel(tc, tab, offs, out):
         tc.tile_pool(name="picked", bufs=blocks) as picked,
     ):
         offsets = held.tile([P, entries // 16], U16, name="offsets")
+        paired = held.tile([P, PAIR * places], F32, name="paired", tag="staging")
         product = held.tile([P, blocks * entries], F32, name="product")
         values = [windows.tile([P, places], F32, name="values") for block in range(blocks)]
         gates = [windows.tile([P, places], F32, name="gates") for block in range(blocks)]
-        opened = [picked.tile([P, entries], F32, name="opened") for block in range(blocks)]
         scaled = [picked.tile([P, entries], F32, name="scaled") for block in range(last)]
         scaled.append(scaled[-1])
 
+        def load(window, side, block):
+            nc.sync.dma_start(window[block][:], table[side, :, block * places : (block + 1) * places])
+
+        nc.sync.dma_start(paired[:], table[0, :, : PAIR * places])
+        nc.sync.dma_start(offsets[:], offs)
         for block in range(blocks):
-            nc.sync.dma_start(values[block][:], table[0, block])
-            if block == 0:
-                nc.sync.dma_start(offsets[:], offs)
-            nc.sync.dma_start(gates[block][:], table[1, block])
+            if block >= PAIR:
+                load(values, 0, block)
+            load(gates, 1, block)
+
+        nc.vector.tensor_copy(values[0][:], paired[:, :places])
+        nc.scalar.activation(values[1][:], paired[:, places:], COPY)
+
+        opened = held.tile([P, blocks * entries], F32, name="opened", tag="staging")
 
         def look_up_values(block, start, end):
             window = values[block][:].indirect(offsets[:, start // 16 : end // 16])
@@ -42,13 +52,9 @@ def tile_lookup_vg_nrmrelu_out_kernel(tc, tab, offs, out):
 
         def gate(block, start, end):
             window = gates[block][:].indirect(offsets[:, start // 16 : end // 16])
-            nc.scalar.activation(opened[block][:, start:end], window, RELU)
-            nc.vector.tensor_tensor(
-                product[:, block * entries + start : block * entries + end],
-                scaled[block][:, start:end],
-                opened[block][:, start:end],
-                MULT,
-            )
+            columns = slice(block * entries + start, block * entries + end)
+            nc.scalar.activation(opened[:, columns], window, RELU)
+            nc.vector.tensor_tensor(product[:, columns], scaled[block][:, start:end], opened[:, columns], MULT)
 
         def store(block, start, end):
             columns = slice(block * entries + start, block * entries + end)
@@ -58,16 +64,13 @@ def tile_lookup_vg_nrmrelu_out_kernel(tc, tab, offs, out):
         for block in range(last - 1):
             look_up_values(block + 1, 0, entries)
             gate(block, 0, entries)
-        store(0, 0, (last - 1) * entries)
+            store(block, 0, entries)
 
-        start = 0
-        for piece in EARLY_PIECES:
-            gate(last - 1, start, start + piece)
-            start += piece
-        look_up_values(last, 0, start)
-        gate(last - 1, start, start + LATE_PIECE)
+        gate(last - 1, 0, half)
+        look_up_values(last, 0, half)
+        gate(last - 1, half, entries)
         store(last - 1, 0, entries)
-        look_up_values(last, start, start + LATE_PIECE)
+        look_up_values(last, half, entries)
 
         start = 0
         for piece in LAST_PIECES:

@@ -6,7 +6,7 @@ SUBTRACT, MULT = mybir.AluOpType.subtract, mybir.AluOpType.mult
 SHIFT, SCALE = 0.125, 1.5
 P = 128
 PAIR = 2
-LAST_PIECES = (320, 256, 192, 128, 128)
+LAST_PIECES = (256, 192, 192, 128, 128, 128)
 
 
 def tile_lookup_vg_nrmrelu_out_kernel(tc, tab, offs, out):
@@ -64,7 +64,7 @@ def tile_lookup_vg_nrmrelu_out_kernel(tc, tab, offs, out):
         for block in range(last - 1):
             look_up_values(block + 1, 0, entries)
             gate(block, 0, entries)
-            store(block, 0, entries)
+        store(0, 0, PAIR * entries)
 
         gate(last - 1, 0, half)
         look_up_values(last, 0, half)

@@ -5,7 +5,6 @@ COPY, RELU = mybir.ActivationFunctionType.Copy, mybir.ActivationFunctionType.Rel
 SUBTRACT, MULT = mybir.AluOpType.subtract, mybir.AluOpType.mult
 SHIFT, SCALE = 0.125, 1.5
 P = 128
-PAIR = 2
 LAST_PIECES = (256, 192, 192, 128, 128, 128)
 
 
@@ -21,59 +20,57 @@ def tile_lookup_vg_nrmrelu_out_kernel(tc, tab, offs, out):
     with (
         tc.tile_pool(name="held", bufs=1) as held,
         tc.tile_pool(name="windows", bufs=blocks) as windows,
-        tc.tile_pool(name="picked", bufs=blocks) as picked,
+        tc.tile_pool(name="picked", bufs=last) as picked,
     ):
         offsets = held.tile([P, entries // 16], U16, name="offsets")
-        paired = held.tile([P, PAIR * places], F32, name="paired", tag="staging")
+        staged = held.tile([P, last * places], F32, name="staged", tag="staging")
         product = held.tile([P, blocks * entries], F32, name="product")
         values = [windows.tile([P, places], F32, name="values") for block in range(blocks)]
         gates = [windows.tile([P, places], F32, name="gates") for block in range(blocks)]
-        scaled = [picked.tile([P, entries], F32, name="scaled") for block in range(last)]
-        scaled.append(scaled[-1])
 
         def load(window, side, block):
             nc.sync.dma_start(window[block][:], table[side, :, block * places : (block + 1) * places])
 
-        nc.sync.dma_start(paired[:], table[0, :, : PAIR * places])
+        nc.sync.dma_start(staged[:], table[0, :, : last * places])
         nc.sync.dma_start(offsets[:], offs)
-        for block in range(blocks):
-            if block >= PAIR:
-                load(values, 0, block)
+        for block in range(last):
             load(gates, 1, block)
+        load(values, 0, last)
+        load(gates, 1, last)
 
-        nc.vector.tensor_copy(values[0][:], paired[:, :places])
-        nc.scalar.activation(values[1][:], paired[:, places:], COPY)
+        nc.vector.tensor_copy(values[0][:], staged[:, :places])
+        nc.scalar.activation(values[1][:], staged[:, places : 2 * places], COPY)
+        nc.vector.tensor_copy(values[2][:], staged[:, 2 * places :])
 
         opened = held.tile([P, blocks * entries], F32, name="opened", tag="staging")
 
-        def look_up_values(block, start, end):
+        def look_up_values(scaled, block, start, end):
             window = values[block][:].indirect(offsets[:, start // 16 : end // 16])
-            nc.vector.tensor_scalar(scaled[block][:, start:end], window, SHIFT, SCALE, op0=SUBTRACT, op1=MULT)
+            nc.vector.tensor_scalar(scaled[:, start:end], window, SHIFT, SCALE, op0=SUBTRACT, op1=MULT)
 
-        def gate(block, start, end):
+        def gate(multiplier, scaled, block, start, end):
             window = gates[block][:].indirect(offsets[:, start // 16 : end // 16])
             columns = slice(block * entries + start, block * entries + end)
             nc.scalar.activation(opened[:, columns], window, RELU)
-            nc.vector.tensor_tensor(product[:, columns], scaled[block][:, start:end], opened[:, columns], MULT)
+            multiplier.tensor_tensor(product[:, columns], scaled[:, start:end], opened[:, columns], MULT)
 
         def store(block, start, end):
             columns = slice(block * entries + start, block * entries + end)
             nc.sync.dma_start(result[:, columns], product[:, columns])
 
-        look_up_values(0, 0, entries)
-        for block in range(last - 1):
-            look_up_values(block + 1, 0, entries)
-            gate(block, 0, entries)
-        store(0, 0, PAIR * entries)
+        for block in range(last):
+            scaled = picked.tile([P, entries], F32, name="scaled")
+            for start in (0, half):
+                look_up_values(scaled, block, start, start + half)
+                gate(nc.gpsimd, scaled, block, start, start + half)
+        store(0, 0, 2 * entries)
+        store(last - 1, 0, half)
+        store(last - 1, half, entries)
 
-        gate(last - 1, 0, half)
-        look_up_values(last, 0, half)
-        gate(last - 1, half, entries)
-        store(last - 1, 0, entries)
-        look_up_values(last, half, entries)
-
+        scaled = picked.tile([P, entries], F32, name="scaled")
+        look_up_values(scaled, last, 0, entries)
         start = 0
         for piece in LAST_PIECES:
-            gate(last, start, start + piece)
+            gate(nc.vector, scaled, last, start, start + piece)
             store(last, start, start + piece)
             start += piece

@@ -5,7 +5,7 @@ COPY, RELU = mybir.ActivationFunctionType.Copy, mybir.ActivationFunctionType.Rel
 SUBTRACT, MULT = mybir.AluOpType.subtract, mybir.AluOpType.mult
 SHIFT, SCALE = 0.125, 1.5
 P = 128
-LAST_PIECES = (256, 192, 192, 128, 128, 128)
+LAST_STORES = (256, 192, 192, 128, 128, 128)
 
 
 def tile_lookup_vg_nrmrelu_out_kernel(tc, tab, offs, out):
@@ -70,7 +70,11 @@ def tile_lookup_vg_nrmrelu_out_kernel(tc, tab, offs, out):
         scaled = picked.tile([P, entries], F32, name="scaled")
         look_up_values(scaled, last, 0, entries)
         start = 0
-        for piece in LAST_PIECES:
-            gate(nc.vector, scaled, last, start, start + piece)
-            store(last, start, start + piece)
-            start += piece
+        for width in LAST_STORES[:-1]:
+            gate(nc.vector, scaled, last, start, start + width)
+            store(last, start, start + width)
+            start += width
+        middle = (start + entries) // 2
+        gate(nc.vector, scaled, last, start, middle)
+        gate(nc.vector, scaled, last, middle, entries)
+        store(last, start, entries)

@@ -5,7 +5,7 @@ COPY, RELU = mybir.ActivationFunctionType.Copy, mybir.ActivationFunctionType.Rel
 SUBTRACT, MULT = mybir.AluOpType.subtract, mybir.AluOpType.mult
 SHIFT, SCALE = 0.125, 1.5
 P = 128
-LAST_STORES = (256, 192, 192, 128, 128, 128)
+LAST_STORES = (256, 256, 192, 192, 128)
 
 
 def tile_lookup_vg_nrmrelu_out_kernel(tc, tab, offs, out):

@@ -63,7 +63,8 @@ def tile_lookup_vg_nrmrelu_out_kernel(tc, tab, offs, out):
             for start in (0, half):
                 look_up_values(scaled, block, start, start + half)
                 gate(nc.gpsimd, scaled, block, start, start + half)
-        store(0, 0, 2 * entries)
+        store(0, 0, entries)
+        store(1, 0, entries)
         store(last - 1, 0, half)
         store(last - 1, half, entries)
 

import concourse.mybir as mybir

F32, U16 = mybir.dt.float32, mybir.dt.uint16
COPY, RELU = mybir.ActivationFunctionType.Copy, mybir.ActivationFunctionType.Relu
SUBTRACT, MULT = mybir.AluOpType.subtract, mybir.AluOpType.mult
SHIFT, SCALE = 0.125, 1.5
P = 128
LAST_STORES = (256, 256, 192, 192, 128)


def tile_lookup_vg_nrmrelu_out_kernel(tc, tab, offs, out):
    nc = tc.nc
    rows, places = tab.shape[1], tab.shape[2]
    entries = out.shape[1]
    half = entries // 2
    blocks = rows // P
    last = blocks - 1
    table = tab.rearrange("h (p b) s -> h p (b s)", b=blocks)
    result = out.rearrange("(p b) n -> p (b n)", b=blocks)
    with (
        tc.tile_pool(name="held", bufs=1) as held,
        tc.tile_pool(name="windows", bufs=blocks) as windows,
        tc.tile_pool(name="picked", bufs=last) as picked,
    ):
        offsets = held.tile([P, entries // 16], U16, name="offsets")
        staged = held.tile([P, last * places], F32, name="staged", tag="staging")
        product = held.tile([P, blocks * entries], F32, name="product")
        values = [windows.tile([P, places], F32, name="values") for block in range(blocks)]
        gates = [windows.tile([P, places], F32, name="gates") for block in range(blocks)]

        def load(window, side, block):
            nc.sync.dma_start(window[block][:], table[side, :, block * places : (block + 1) * places])

        nc.sync.dma_start(staged[:], table[0, :, : last * places])
        nc.sync.dma_start(offsets[:], offs)
        for block in range(last):
            load(gates, 1, block)
        load(values, 0, last)
        load(gates, 1, last)

        nc.vector.tensor_copy(values[0][:], staged[:, :places])
        nc.scalar.activation(values[1][:], staged[:, places : 2 * places], COPY)
        nc.vector.tensor_copy(values[2][:], staged[:, 2 * places :])

        opened = held.tile([P, blocks * entries], F32, name="opened", tag="staging")

        def look_up_values(scaled, block, start, end):
            window = values[block][:].indirect(offsets[:, start // 16 : end // 16])
            nc.vector.tensor_scalar(scaled[:, start:end], window, SHIFT, SCALE, op0=SUBTRACT, op1=MULT)

        def gate(multiplier, scaled, block, start, end):
            window = gates[block][:].indirect(offsets[:, start // 16 : end // 16])
            columns = slice(block * entries + start, block * entries + end)
            nc.scalar.activation(opened[:, columns], window, RELU)
            multiplier.tensor_tensor(product[:, columns], scaled[:, start:end], opened[:, columns], MULT)

        def store(block, start, end):
            columns = slice(block * entries + start, block * entries + end)
            nc.sync.dma_start(result[:, columns], product[:, columns])

        for block in range(last):
            scaled = picked.tile([P, entries], F32, name="scaled")
            for start in (0, half):
                look_up_values(scaled, block, start, start + half)
                gate(nc.gpsimd, scaled, block, start, start + half)
        store(0, 0, entries)
        store(1, 0, entries)
        store(last - 1, 0, half)
        store(last - 1, half, entries)

        scaled = picked.tile([P, entries], F32, name="scaled")
        look_up_values(scaled, last, 0, entries)
        start = 0
        for width in LAST_STORES[:-1]:
            gate(nc.vector, scaled, last, start, start + width)
            store(last, start, start + width)
            start += width
        middle = (start + entries) // 2
        gate(nc.vector, scaled, last, start, middle)
        gate(nc.vector, scaled, last, middle, entries)
        store(last, start, entries)
